import numpy as np
import ml_dtypes


def mxq(x, axis, fmt="e4m3"):
    dtype, down = {"e4m3": (ml_dtypes.float8_e4m3fn, 7), "e5m2": (ml_dtypes.float8_e5m2, 14)}[fmt]
    v = np.moveaxis(np.asarray(x, np.float32).astype(ml_dtypes.bfloat16).astype(np.float64), axis, -1)
    blocks = v.reshape(v.shape[:-1] + (-1, 32))
    amax = np.abs(blocks).max(-1, keepdims=True)
    byte = np.maximum(np.where(amax > 0, np.frexp(amax)[1] - 1 + 127, 0) - down, 1)
    scale = np.exp2(byte - 127.0)
    codes = (blocks / scale).astype(np.float32).astype(dtype).astype(np.float64)
    return np.moveaxis((codes * scale).reshape(v.shape), -1, axis)


WIDE = False


def mx_kscale(k):
    if not WIDE:
        return np.ones(k)
    levels = np.array([30, -30])
    if k % 512:
        return np.exp2(np.random.permutation(np.resize(levels, k // 32))).repeat(32)
    a = np.empty((k // 512, 16))
    for p in range(k // 512):
        a[p, :8] = np.random.permutation(np.resize(levels, 8))
        for g in range(8):
            far = levels[np.abs(levels - a[p, g]) >= 10]
            a[p, g + 8] = far[np.random.randint(len(far))]
    return np.exp2(a.ravel()).repeat(32)


def f64(x):
    return np.asarray(x).astype(np.float64)


def striped(idx):
    return np.tile(np.asarray(idx).reshape(-1, 16).T, (8, 1)).astype(np.uint16)


def unstriped(offs):
    return offs[:16].T.reshape(-1).astype(np.int64)


E2M1 = np.array([0.0, 0.5, 1.0, 1.5, 2.0, 3.0, 4.0, 6.0, -0.0, -0.5, -1.0, -1.5, -2.0, -3.0, -4.0, -6.0])


def pack_weight(w, fmt):
    k, n = w.shape
    w = f64(np.asarray(w, np.float32).astype(ml_dtypes.bfloat16)).reshape(k // 32, 32, n)
    amax = np.abs(w).max(1)
    if fmt in ("e4m3", "e5m2"):
        byte = np.frexp(amax)[1] - 1 + 127 - (7 if fmt == "e4m3" else 14)
    else:
        mant, ex = np.frexp(amax / 6.0)
        byte = np.where(mant > 0.5, ex, ex - 1) + 127
    byte = np.clip(np.where(amax > 0, byte, 1), 1, 254)
    scaled = (w * np.exp2(127.0 - byte)[:, None, :]).reshape(k, n).astype(np.float32)
    by_word = np.ascontiguousarray(scaled.reshape(k // 512, 128, 4, n).transpose(0, 1, 3, 2))
    if fmt in ("e4m3", "e5m2"):
        words = by_word.astype(ml_dtypes.float8_e4m3fn if fmt == "e4m3" else ml_dtypes.float8_e5m2).view(np.uint8)
    else:
        c = by_word.astype(ml_dtypes.float4_e2m1fn).view(np.uint8) & 0xF
        words = (c[..., 0::2] | (c[..., 1::2] << 4)).reshape(k // 512, 128, 2 * n)
    return np.ascontiguousarray(words), np.ascontiguousarray(byte.astype(np.uint8).reshape(k // 512, 16, n))


def unpack_weight(words, scales, fmt):
    g, _, n = scales.shape
    words = np.ascontiguousarray(words).reshape(g, 128, n, -1)
    if fmt in ("e4m3", "e5m2"):
        vals = words.view(ml_dtypes.float8_e4m3fn if fmt == "e4m3" else ml_dtypes.float8_e5m2).astype(np.float64)
    else:
        nib = np.empty((g, 128, n, 4), np.uint8)
        nib[..., 0::2] = words & 0xF
        nib[..., 1::2] = words >> 4
        vals = E2M1[nib]
    vals = vals * np.repeat(np.exp2(scales.astype(np.float64) - 127.0), 8, axis=1)[..., None]
    return vals.transpose(0, 1, 3, 2).reshape(g * 512, n)


K, T, J, R, X, O, N, E = 512, 1024, 256, 512, 1024, 128, 256, 512


def setup_inputs():
    n = np.random.standard_normal
    idx = np.random.permutation(T)[:J]
    idx2 = np.random.permutation(J)[:O]
    idx3 = np.random.permutation(X)[:O]
    idx4 = np.random.permutation(X)[:O]
    idx5 = np.random.permutation(T)[:O]
    idx6 = np.random.permutation(E)[:O]
    idx7 = np.random.permutation(E)[:O]
    fk = mx_kscale(K)
    fr = mx_kscale(R)
    xtp = pack_weight(n((K, T)) / fk[:, None], "e5m2")
    wp = pack_weight(n((K, R)) * 1 / np.sqrt(K) * fk[:, None] * fr, "e2m1")
    wbp = pack_weight(n((R, N)) * 1 / np.sqrt(R) / fr[:, None], "e2m1")
    wsp = pack_weight(n((K, N)) * 1 / np.sqrt(K) * fk[:, None], "e2m1")
    return {
        "xt_words": xtp[0],
        "xt_scales": xtp[1],
        "w_words": wp[0],
        "w_scales": wp[1],
        "tb": (n((R, X)) * 1.0).astype(np.float32),
        "wb_words": wbp[0],
        "wb_scales": wbp[1],
        "ws_words": wsp[0],
        "ws_scales": wsp[1],
        "offs": striped(idx),
        "offs2": striped(idx2),
        "offs3": striped(idx3),
        "offs4": striped(idx4),
        "offs5": striped(idx5),
        "offs6": striped(idx6),
        "offs7": striped(idx7),
    }


def reference(xt_words, xt_scales, w_words, w_scales, tb, wb_words, wb_scales, ws_words, ws_scales, offs, offs2, offs3, offs4, offs5, offs6, offs7):
    idx = unstriped(offs)
    idx2 = unstriped(offs2)
    idx3 = unstriped(offs3)
    idx4 = unstriped(offs4)
    idx5 = unstriped(offs5)
    idx6 = unstriped(offs6)
    idx7 = unstriped(offs7)
    xtu = unpack_weight(xt_words, xt_scales, "e5m2")
    wu = unpack_weight(w_words, w_scales, "e2m1")
    wbu = unpack_weight(wb_words, wb_scales, "e2m1")
    wsu = unpack_weight(ws_words, ws_scales, "e2m1")
    xtidxg = xtu[:, idx]
    a = wu.T @ xtidxg
    la = a[:, 0:1]
    la2 = a[:, 128:129]
    hid = np.maximum(np.minimum(a[:, idx2], f64(tb)[:, idx3] * la), f64(tb)[:, idx4] * la2)
    hidq = mxq(hid, 0, "e4m3")
    xtidx5g = xtu[:, idx5]
    p = wbu.T @ hidq + wsu.T @ xtidx5g
    pa = np.zeros((N, E))
    pa[:, idx6] = p
    pb = np.zeros((N, E))
    pb[:, idx7] = p
    y = pa + pb
    return y

@@ -1,0 +1,157 @@
+from contextlib import ExitStack
+
+import concourse.mybir as mybir
+
+K, T, J, R, X, O, N, E = 512, 1024, 256, 512, 1024, 128, 256, 512
+FLOPS = 2 * K * R * J + 2 * R * N * O + 2 * K * N * O
+
+F32 = mybir.dt.float32
+BF16 = mybir.dt.bfloat16
+I32 = mybir.dt.int32
+U32 = mybir.dt.uint32
+U16 = mybir.dt.uint16
+U8 = mybir.dt.uint8
+E4M3 = mybir.dt.float8_e4m3fn_x4
+E5M2 = mybir.dt.float8_e5m2_x4
+E2M1 = mybir.dt.float4_e2m1fn_x4
+COPY = mybir.ActivationFunctionType.Copy
+ALU = mybir.AluOpType
+
+P = 128
+PACK = 4
+QUADS = 4
+
+
+def tile_list_leadbounds_solo_further_pagetwice_kernel(
+    tc, xt_words, xt_scales, w_words, w_scales, tb, wb_words, wb_scales, ws_words, ws_scales,
+    offs, offs2, offs3, offs4, offs5, offs6, offs7, out,
+):
+    nc = tc.nc
+    with ExitStack() as ctx:
+        sb = ctx.enter_context(tc.tile_pool(name="sb", bufs=1))
+        ps = ctx.enter_context(tc.psum_pool(name="ps", bufs=1))
+
+        def tile(name, shape, dtype):
+            return sb.tile(shape, dtype, name=name, align_bytes=64)
+
+        def load_list(name, src):
+            t = tile(name, list(src.shape), U16)
+            nc.sync.dma_start(t[:], src)
+            return t
+
+        xt_plane = tile("xt_plane", [P, T], U8)
+        w_plane = tile("w_plane", [P, R], U8)
+        ws_plane = tile("ws_plane", [P, N], U8)
+        wb_plane = tile("wb_plane", [P, N], U8)
+        for plane in (xt_plane, w_plane, ws_plane, wb_plane):
+            nc.gpsimd.memset(plane[:].bitcast(I32), 0)
+        pages = [[tile("page%d%d" % (h, s), [P, E], F32) for s in range(2)] for h in range(2)]
+        for h in range(2):
+            for s in range(2):
+                nc.vector.memset(pages[h][s][:], 0.0)
+
+        def load_plane(queue, plane, scales):
+            for q in range(QUADS):
+                queue.dma_start(
+                    out=plane[32 * q : 32 * q + 4, :].bitcast(I32), in_=scales[0, 4 * q : 4 * q + 4, :].bitcast(I32)
+                )
+
+        w_stage = tile("w_stage", [PACK, QUADS, R // 4], I32)
+        nc.sync.dma_start(out=w_stage[:], in_=w_scales[0].bitcast(I32).rearrange("(q r) c -> r q c", r=4))
+        l1 = load_list("l1", offs)
+        xw = tile("xw", [P, T], U32)
+        nc.sync.dma_start(out=xw[:].bitcast(I32), in_=xt_words[0].rearrange("p n t -> p (n t)").bitcast(I32))
+        ww = tile("ww", [P, 2 * R], U8)
+        nc.sync.dma_start(out=ww[:].bitcast(I32), in_=w_words[0].bitcast(I32))
+        load_plane(nc.sync, xt_plane, xt_scales)
+        tb_rows = tb.rearrange("(p t) x -> t p x", t=PACK)
+        tbt = [tile("tb%d" % t, [P, X], F32) for t in range(PACK)]
+        for t in range(2):
+            nc.sync.dma_start(out=tbt[t][:], in_=tb_rows[t])
+        l3 = load_list("l3", offs3)
+        l4 = load_list("l4", offs4)
+        l2 = load_list("l2", offs2)
+        l5 = load_list("l5", offs5)
+        for t in range(2, PACK):
+            nc.sync.dma_start(out=tbt[t][:], in_=tb_rows[t])
+        wsw = tile("wsw", [P, 2 * N], U8)
+        wbw = tile("wbw", [P, 2 * N], U8)
+        nc.sync.dma_start(out=wsw[:].bitcast(I32), in_=ws_words[0].bitcast(I32))
+        nc.sync.dma_start(out=wbw[:].bitcast(I32), in_=wb_words[0].bitcast(I32))
+        load_plane(nc.sync, wb_plane, wb_scales)
+        load_plane(nc.gpsimd, ws_plane, ws_scales)
+        l6 = load_list("l6", offs6)
+        l7 = load_list("l7", offs7)
+
+        wd = tile("wd", [P, 2 * R], U8)
+        nc.scalar.copy(
+            out=wd[:].bitcast(U16).rearrange("p (t m) -> p t m", t=PACK),
+            in_=ww[:].bitcast(U16).rearrange("p (m t) -> p t m", t=PACK),
+        )
+        for q in (1, 2, 3, 0):
+            nc.vector.tensor_copy(w_plane[32 * q : 32 * q + 4, :].bitcast(I32), w_stage[:, q, :])
+        xg_s = tile("xg_s", [P, J], U8)
+        nc.vector.tensor_copy(xg_s[:], xt_plane[:].indirect(l1[:]))
+        xg = tile("xg", [P, J], U32)
+        nc.vector.tensor_copy(xg[:], xw[:].indirect(l1[:]))
+        wd_s = [tile("wd_s%d" % t, [P, P], U8) for t in range(PACK)]
+        a_ps = [ps.tile([P, J], F32, name="a_ps%d" % t) for t in range(PACK)]
+        for t in range(PACK):
+            nc.vector.tensor_copy(wd_s[t][:], w_plane[:].rearrange("p (m t) -> p t m", t=PACK)[:, t, :])
+            nc.tensor.matmul_mx(
+                out=a_ps[t][:], lhsT=wd[:, 2 * P * t : 2 * P * (t + 1)].bitcast(E2M1), lhsT_scale=wd_s[t][:],
+                rhs=xg[:].bitcast(E5M2), rhs_scale=xg_s[:], start=True, stop=True,
+            )
+
+        x5_s = tile("x5_s", [P, O], U8)
+        nc.vector.tensor_copy(x5_s[:], xt_plane[:].indirect(l5[:]))
+        x5 = tile("x5", [P, O], U32)
+        nc.vector.tensor_copy(x5[:], xw[:].indirect(l5[:]))
+        p_ps = [ps.tile([P, O], F32, name="p_ps%d" % h) for h in range(2)]
+        for h in range(2):
+            nc.tensor.matmul_mx(
+                out=p_ps[h][:], lhsT=wsw[:, 2 * P * h : 2 * P * (h + 1)].bitcast(E2M1),
+                lhsT_scale=ws_plane[:, P * h : P * (h + 1)],
+                rhs=x5[:].bitcast(E5M2), rhs_scale=x5_s[:], start=True, stop=False,
+            )
+
+        groups = [(0, 3), (3, 4)]
+        hid = tile("hid", [P, O, PACK], BF16)
+        for t0, t1 in groups:
+            n_t = t1 - t0
+            picked = tile("picked%d" % t0, [P, n_t, O], F32)
+            upper = tile("upper%d" % t0, [P, n_t, O], F32)
+            lower = tile("lower%d" % t0, [P, n_t, O], F32)
+            cut = tile("cut%d" % t0, [P, n_t, O], F32)
+            for t in range(t0, t1):
+                a_sb = tile("a_sb%d" % t, [P, J], F32)
+                if t < 2:
+                    nc.scalar.activation(a_sb[:], a_ps[t][:], COPY)
+                else:
+                    nc.vector.tensor_copy(a_sb[:], a_ps[t][:])
+                nc.scalar.activation(upper[:, t - t0, :], tbt[t][:].indirect(l3[:]), COPY, scale=a_sb[:, 0:1])
+                nc.scalar.activation(lower[:, t - t0, :], tbt[t][:].indirect(l4[:]), COPY, scale=a_sb[:, 128:129])
+                nc.vector.tensor_copy(picked[:, t - t0, :], a_sb[:].indirect(l2[:]))
+            nc.vector.tensor_tensor(cut[:], picked[:], upper[:], ALU.min)
+            nc.vector.tensor_tensor(
+                hid[:, :, t0:t1], cut[:].rearrange("p t o -> p o t"), lower[:].rearrange("p t o -> p o t"), ALU.max
+            )
+        hq = tile("hq", [P, O], U32)
+        hq_s = tile("hq_s", [P, O], U8)
+        nc.vector.quantize_mx(out=hq[:].bitcast(E4M3), scales=hq_s[:], in_=hid[:].rearrange("p o t -> p (o t)"))
+        p_sb = [tile("p_sb%d" % h, [P, O], F32) for h in range(2)]
+        for h in range(2):
+            nc.tensor.matmul_mx(
+                out=p_ps[h][:], lhsT=wbw[:, 2 * P * h : 2 * P * (h + 1)].bitcast(E2M1),
+                lhsT_scale=wb_plane[:, P * h : P * (h + 1)],
+                rhs=hq[:].bitcast(E4M3), rhs_scale=hq_s[:], start=False, stop=True,
+            )
+        nc.vector.tensor_copy(p_sb[0][:], p_ps[0][:])
+        nc.scalar.activation(p_sb[1][:], p_ps[1][:], COPY)
+        for h in range(2):
+            nc.vector.tensor_copy(pages[h][0][:].indirect(l6[:]), p_sb[h][:])
+            nc.scalar.activation(pages[h][1][:].indirect(l7[:]), p_sb[h][:], COPY)
+            res = tile("res%d" % h, [P, E], F32)
+            for c0, c1 in ([(0, E)] if h == 0 else [(0, E // 2), (E // 2, E)]):
+                nc.vector.tensor_tensor(res[:, c0:c1], pages[h][0][:, c0:c1], pages[h][1][:, c0:c1], ALU.add)
+                nc.sync.dma_start(out=out[P * h : P * (h + 1), c0:c1], in_=res[:, c0:c1])

@@ -40,37 +40,35 @@ def tile_list_leadbounds_solo_further_pagetwice_kernel(
             return t
 
         xt_plane = tile("xt_plane", [P, T], U8)
-        w_plane = tile("w_plane", [P, R], U8)
-        ws_plane = tile("ws_plane", [P, N], U8)
-        wb_plane = tile("wb_plane", [P, N], U8)
-        for plane in (xt_plane, w_plane, ws_plane, wb_plane):
-            nc.gpsimd.memset(plane[:].bitcast(I32), 0)
+        w_plane = tile("w_plane", [P, R + 2 * N], U8)
+        nc.vector.memset(xt_plane[:].bitcast(I32), 0)
+        nc.vector.memset(w_plane[:].bitcast(I32), 0)
         pages = [[tile("page%d%d" % (h, s), [P, E], F32) for s in range(2)] for h in range(2)]
         for h in range(2):
             for s in range(2):
-                nc.vector.memset(pages[h][s][:], 0.0)
+                nc.vector.memset(pages[h][s][:].bitcast(I32), 0)
 
-        def load_plane(queue, plane, scales):
-            for q in range(QUADS):
-                queue.dma_start(
-                    out=plane[32 * q : 32 * q + 4, :].bitcast(I32), in_=scales[0, 4 * q : 4 * q + 4, :].bitcast(I32)
-                )
-
-        w_stage = tile("w_stage", [PACK, QUADS, R // 4], I32)
-        nc.sync.dma_start(out=w_stage[:], in_=w_scales[0].bitcast(I32).rearrange("(q r) c -> r q c", r=4))
+        stage = tile("stage", [PACK, QUADS, (R + 2 * N) // 4], I32)
+        for scales, c0, c1 in ((w_scales, 0, R), (ws_scales, R, R + N), (wb_scales, R + N, R + 2 * N)):
+            nc.sync.dma_start(
+                out=stage[:, :, c0 // 4 : c1 // 4], in_=scales[0].bitcast(I32).rearrange("(q r) c -> r q c", r=4)
+            )
         l1 = load_list("l1", offs)
         xw = tile("xw", [P, T], U32)
         nc.sync.dma_start(out=xw[:].bitcast(I32), in_=xt_words[0].rearrange("p n t -> p (n t)").bitcast(I32))
+        for q in range(QUADS):
+            nc.sync.dma_start(
+                out=xt_plane[32 * q : 32 * q + 4, :].bitcast(I32), in_=xt_scales[0, 4 * q : 4 * q + 4, :].bitcast(I32)
+            )
         ww = tile("ww", [P, 2 * R], U8)
         nc.sync.dma_start(out=ww[:].bitcast(I32), in_=w_words[0].bitcast(I32))
-        load_plane(nc.sync, xt_plane, xt_scales)
         tb_rows = tb.rearrange("(p t) x -> t p x", t=PACK)
         tbt = [tile("tb%d" % t, [P, X], F32) for t in range(PACK)]
-        for t in range(2):
-            nc.sync.dma_start(out=tbt[t][:], in_=tb_rows[t])
+        nc.sync.dma_start(out=tbt[0][:], in_=tb_rows[0])
         l3 = load_list("l3", offs3)
         l4 = load_list("l4", offs4)
         l2 = load_list("l2", offs2)
+        nc.sync.dma_start(out=tbt[1][:], in_=tb_rows[1])
         l5 = load_list("l5", offs5)
         for t in range(2, PACK):
             nc.sync.dma_start(out=tbt[t][:], in_=tb_rows[t])
@@ -78,8 +76,6 @@ def tile_list_leadbounds_solo_further_pagetwice_kernel(
         wbw = tile("wbw", [P, 2 * N], U8)
         nc.sync.dma_start(out=wsw[:].bitcast(I32), in_=ws_words[0].bitcast(I32))
         nc.sync.dma_start(out=wbw[:].bitcast(I32), in_=wb_words[0].bitcast(I32))
-        load_plane(nc.sync, wb_plane, wb_scales)
-        load_plane(nc.gpsimd, ws_plane, ws_scales)
         l6 = load_list("l6", offs6)
         l7 = load_list("l7", offs7)
 
@@ -89,33 +85,21 @@ def tile_list_leadbounds_solo_further_pagetwice_kernel(
             in_=ww[:].bitcast(U16).rearrange("p (m t) -> p t m", t=PACK),
         )
         for q in (1, 2, 3, 0):
-            nc.vector.tensor_copy(w_plane[32 * q : 32 * q + 4, :].bitcast(I32), w_stage[:, q, :])
-        xg_s = tile("xg_s", [P, J], U8)
-        nc.vector.tensor_copy(xg_s[:], xt_plane[:].indirect(l1[:]))
+            nc.vector.tensor_copy(w_plane[32 * q : 32 * q + 4, :].bitcast(I32), stage[:, q, :])
         xg = tile("xg", [P, J], U32)
         nc.vector.tensor_copy(xg[:], xw[:].indirect(l1[:]))
+        xg_s = tile("xg_s", [P, J], U8)
+        nc.vector.tensor_copy(xg_s[:], xt_plane[:].indirect(l1[:]))
         wd_s = [tile("wd_s%d" % t, [P, P], U8) for t in range(PACK)]
         a_ps = [ps.tile([P, J], F32, name="a_ps%d" % t) for t in range(PACK)]
         for t in range(PACK):
-            nc.vector.tensor_copy(wd_s[t][:], w_plane[:].rearrange("p (m t) -> p t m", t=PACK)[:, t, :])
+            nc.vector.tensor_copy(wd_s[t][:], w_plane[:, :R].rearrange("p (m t) -> p t m", t=PACK)[:, t, :])
             nc.tensor.matmul_mx(
                 out=a_ps[t][:], lhsT=wd[:, 2 * P * t : 2 * P * (t + 1)].bitcast(E2M1), lhsT_scale=wd_s[t][:],
                 rhs=xg[:].bitcast(E5M2), rhs_scale=xg_s[:], start=True, stop=True,
             )
 
-        x5_s = tile("x5_s", [P, O], U8)
-        nc.vector.tensor_copy(x5_s[:], xt_plane[:].indirect(l5[:]))
-        x5 = tile("x5", [P, O], U32)
-        nc.vector.tensor_copy(x5[:], xw[:].indirect(l5[:]))
-        p_ps = [ps.tile([P, O], F32, name="p_ps%d" % h) for h in range(2)]
-        for h in range(2):
-            nc.tensor.matmul_mx(
-                out=p_ps[h][:], lhsT=wsw[:, 2 * P * h : 2 * P * (h + 1)].bitcast(E2M1),
-                lhsT_scale=ws_plane[:, P * h : P * (h + 1)],
-                rhs=x5[:].bitcast(E5M2), rhs_scale=x5_s[:], start=True, stop=False,
-            )
-
-        groups = [(0, 3), (3, 4)]
+        groups = [(0, 2), (2, 4)]
         hid = tile("hid", [P, O, PACK], BF16)
         for t0, t1 in groups:
             n_t = t1 - t0
@@ -132,26 +116,43 @@ def tile_list_leadbounds_solo_further_pagetwice_kernel(
                 nc.scalar.activation(upper[:, t - t0, :], tbt[t][:].indirect(l3[:]), COPY, scale=a_sb[:, 0:1])
                 nc.scalar.activation(lower[:, t - t0, :], tbt[t][:].indirect(l4[:]), COPY, scale=a_sb[:, 128:129])
                 nc.vector.tensor_copy(picked[:, t - t0, :], a_sb[:].indirect(l2[:]))
-            nc.vector.tensor_tensor(cut[:], picked[:], upper[:], ALU.min)
+                if t0 > 0:
+                    nc.vector.tensor_tensor(cut[:, t - t0, :], picked[:, t - t0, :], upper[:, t - t0, :], ALU.min)
+            if t0 == 0:
+                nc.vector.tensor_tensor(cut[:], picked[:], upper[:], ALU.min)
             nc.vector.tensor_tensor(
                 hid[:, :, t0:t1], cut[:].rearrange("p t o -> p o t"), lower[:].rearrange("p t o -> p o t"), ALU.max
             )
         hq = tile("hq", [P, O], U32)
         hq_s = tile("hq_s", [P, O], U8)
         nc.vector.quantize_mx(out=hq[:].bitcast(E4M3), scales=hq_s[:], in_=hid[:].rearrange("p o t -> p (o t)"))
-        p_sb = [tile("p_sb%d" % h, [P, O], F32) for h in range(2)]
+
+        x5_s = tile("x5_s", [P, O], U8)
+        nc.vector.tensor_copy(x5_s[:], xt_plane[:].indirect(l5[:]))
+        x5 = tile("x5", [P, O], U32)
+        nc.vector.tensor_copy(x5[:], xw[:].indirect(l5[:]))
+        p_ps = [ps.tile([P, O], F32, name="p_ps%d" % h) for h in range(2)]
+        for h in range(2):
+            nc.tensor.matmul_mx(
+                out=p_ps[h][:], lhsT=wsw[:, 2 * P * h : 2 * P * (h + 1)].bitcast(E2M1),
+                lhsT_scale=w_plane[:, R + P * h : R + P * (h + 1)],
+                rhs=x5[:].bitcast(E5M2), rhs_scale=x5_s[:], start=True, stop=False,
+            )
         for h in range(2):
             nc.tensor.matmul_mx(
                 out=p_ps[h][:], lhsT=wbw[:, 2 * P * h : 2 * P * (h + 1)].bitcast(E2M1),
-                lhsT_scale=wb_plane[:, P * h : P * (h + 1)],
+                lhsT_scale=w_plane[:, R + N + P * h : R + N + P * (h + 1)],
                 rhs=hq[:].bitcast(E4M3), rhs_scale=hq_s[:], start=False, stop=True,
             )
+        p_sb = [tile("p_sb%d" % h, [P, O], F32) for h in range(2)]
+        res = [tile("res%d" % h, [P, E], F32) for h in range(2)]
         nc.vector.tensor_copy(p_sb[0][:], p_ps[0][:])
-        nc.scalar.activation(p_sb[1][:], p_ps[1][:], COPY)
-        for h in range(2):
-            nc.vector.tensor_copy(pages[h][0][:].indirect(l6[:]), p_sb[h][:])
-            nc.scalar.activation(pages[h][1][:].indirect(l7[:]), p_sb[h][:], COPY)
-            res = tile("res%d" % h, [P, E], F32)
-            for c0, c1 in ([(0, E)] if h == 0 else [(0, E // 2), (E // 2, E)]):
-                nc.vector.tensor_tensor(res[:, c0:c1], pages[h][0][:, c0:c1], pages[h][1][:, c0:c1], ALU.add)
-                nc.sync.dma_start(out=out[P * h : P * (h + 1), c0:c1], in_=res[:, c0:c1])
+        nc.vector.tensor_copy(p_sb[1][:], p_ps[1][:])
+        nc.vector.tensor_copy(pages[0][0][:].indirect(l6[:]), p_sb[0][:])
+        nc.scalar.activation(pages[0][1][:].indirect(l7[:]), p_sb[0][:], COPY)
+        nc.vector.tensor_copy(pages[1][0][:].indirect(l6[:, 0:4]), p_sb[1][:, 0:64])
+        nc.scalar.activation(pages[1][1][:].indirect(l7[:]), p_sb[1][:], COPY)
+        nc.scalar.activation(pages[1][0][:].indirect(l6[:, 4:8]), p_sb[1][:, 64:128], COPY)
+        for h, c0, c1 in ((0, 0, E), (1, 0, E // 2), (1, E // 2, E)):
+            nc.vector.tensor_tensor(res[h][:, c0:c1], pages[h][0][:, c0:c1], pages[h][1][:, c0:c1], ALU.add)
+            nc.sync.dma_start(out=out[P * h : P * (h + 1), c0:c1], in_=res[h][:, c0:c1])

@@ -40,50 +40,57 @@ def tile_list_leadbounds_solo_further_pagetwice_kernel(
             return t
 
         xt_plane = tile("xt_plane", [P, T], U8)
-        w_plane = tile("w_plane", [P, R + 2 * N], U8)
+        w_plane = tile("w_plane", [P, R], U8)
+        out_plane = tile("out_plane", [P, 2 * N], U8)
         nc.vector.memset(xt_plane[:].bitcast(I32), 0)
         nc.vector.memset(w_plane[:].bitcast(I32), 0)
+        nc.vector.memset(out_plane[:].bitcast(I32), 0)
         pages = [[tile("page%d%d" % (h, s), [P, E], F32) for s in range(2)] for h in range(2)]
         for h in range(2):
             for s in range(2):
                 nc.vector.memset(pages[h][s][:].bitcast(I32), 0)
 
-        stage = tile("stage", [PACK, QUADS, (R + 2 * N) // 4], I32)
-        for scales, c0, c1 in ((w_scales, 0, R), (ws_scales, R, R + N), (wb_scales, R + N, R + 2 * N)):
+        def load_rows(plane, scales, q):
             nc.sync.dma_start(
-                out=stage[:, :, c0 // 4 : c1 // 4], in_=scales[0].bitcast(I32).rearrange("(q r) c -> r q c", r=4)
+                out=plane[32 * q : 32 * q + 4, :].bitcast(I32), in_=scales[0, 4 * q : 4 * q + 4, :].bitcast(I32)
             )
+
+        stage = tile("stage", [PACK, QUADS, R // 4], I32)
+        nc.sync.dma_start(out=stage[:], in_=w_scales[0].bitcast(I32).rearrange("(q r) c -> r q c", r=4))
         l1 = load_list("l1", offs)
         xw = tile("xw", [P, T], U32)
         nc.sync.dma_start(out=xw[:].bitcast(I32), in_=xt_words[0].rearrange("p n t -> p (n t)").bitcast(I32))
-        for q in range(QUADS):
-            nc.sync.dma_start(
-                out=xt_plane[32 * q : 32 * q + 4, :].bitcast(I32), in_=xt_scales[0, 4 * q : 4 * q + 4, :].bitcast(I32)
-            )
         ww = tile("ww", [P, 2 * R], U8)
         nc.sync.dma_start(out=ww[:].bitcast(I32), in_=w_words[0].bitcast(I32))
+        for q in range(QUADS):
+            load_rows(xt_plane[:], xt_scales, q)
         tb_rows = tb.rearrange("(p t) x -> t p x", t=PACK)
         tbt = [tile("tb%d" % t, [P, X], F32) for t in range(PACK)]
         nc.sync.dma_start(out=tbt[0][:], in_=tb_rows[0])
+        l5 = load_list("l5", offs5)
+        nc.sync.dma_start(out=tbt[1][:], in_=tb_rows[1])
         l3 = load_list("l3", offs3)
         l4 = load_list("l4", offs4)
         l2 = load_list("l2", offs2)
-        nc.sync.dma_start(out=tbt[1][:], in_=tb_rows[1])
-        l5 = load_list("l5", offs5)
-        for t in range(2, PACK):
-            nc.sync.dma_start(out=tbt[t][:], in_=tb_rows[t])
         wsw = tile("wsw", [P, 2 * N], U8)
         wbw = tile("wbw", [P, 2 * N], U8)
         nc.sync.dma_start(out=wsw[:].bitcast(I32), in_=ws_words[0].bitcast(I32))
         nc.sync.dma_start(out=wbw[:].bitcast(I32), in_=wb_words[0].bitcast(I32))
+        nc.sync.dma_start(out=tbt[2][:], in_=tb_rows[2])
+        load_rows(out_plane[:, :N], ws_scales, 0)
+        nc.sync.dma_start(out=tbt[3][:], in_=tb_rows[3])
+        for q in range(1, QUADS):
+            load_rows(out_plane[:, :N], ws_scales, q)
+        for q in range(QUADS):
+            load_rows(out_plane[:, N:], wb_scales, q)
         l6 = load_list("l6", offs6)
         l7 = load_list("l7", offs7)
 
-        wd = tile("wd", [P, 2 * R], U8)
-        nc.scalar.copy(
-            out=wd[:].bitcast(U16).rearrange("p (t m) -> p t m", t=PACK),
-            in_=ww[:].bitcast(U16).rearrange("p (m t) -> p t m", t=PACK),
-        )
+        wd = [tile("wd%d" % t, [P, 2 * P], U8) for t in range(PACK)]
+        for t in range(PACK):
+            nc.scalar.copy(
+                out=wd[t][:].bitcast(U16), in_=ww[:].bitcast(U16).rearrange("p (m t) -> p t m", t=PACK)[:, t, :]
+            )
         for q in (1, 2, 3, 0):
             nc.vector.tensor_copy(w_plane[32 * q : 32 * q + 4, :].bitcast(I32), stage[:, q, :])
         xg = tile("xg", [P, J], U32)
@@ -95,12 +102,18 @@ def tile_list_leadbounds_solo_further_pagetwice_kernel(
         for t in range(PACK):
             nc.vector.tensor_copy(wd_s[t][:], w_plane[:, :R].rearrange("p (m t) -> p t m", t=PACK)[:, t, :])
             nc.tensor.matmul_mx(
-                out=a_ps[t][:], lhsT=wd[:, 2 * P * t : 2 * P * (t + 1)].bitcast(E2M1), lhsT_scale=wd_s[t][:],
+                out=a_ps[t][:], lhsT=wd[t][:].bitcast(E2M1), lhsT_scale=wd_s[t][:],
                 rhs=xg[:].bitcast(E5M2), rhs_scale=xg_s[:], start=True, stop=True,
             )
 
+        x5_s = tile("x5_s", [P, O], U8)
+        nc.vector.tensor_copy(x5_s[:], xt_plane[:].indirect(l5[:]))
+        x5 = tile("x5", [P, O], U32)
+        nc.vector.tensor_copy(x5[:], xw[:].indirect(l5[:]))
+
         groups = [(0, 2), (2, 4)]
-        hid = tile("hid", [P, O, PACK], BF16)
+        half = O // 2
+        hid = [tile("hid%d" % c, [P, half, PACK], BF16) for c in range(2)]
         for t0, t1 in groups:
             n_t = t1 - t0
             picked = tile("picked%d" % t0, [P, n_t, O], F32)
@@ -120,39 +133,44 @@ def tile_list_leadbounds_solo_further_pagetwice_kernel(
                     nc.vector.tensor_tensor(cut[:, t - t0, :], picked[:, t - t0, :], upper[:, t - t0, :], ALU.min)
             if t0 == 0:
                 nc.vector.tensor_tensor(cut[:], picked[:], upper[:], ALU.min)
-            nc.vector.tensor_tensor(
-                hid[:, :, t0:t1], cut[:].rearrange("p t o -> p o t"), lower[:].rearrange("p t o -> p o t"), ALU.max
-            )
+            for c in range(2):
+                cols = slice(half * c, half * (c + 1))
+                nc.vector.tensor_tensor(
+                    hid[c][:, :, t0:t1],
+                    cut[:, :, cols].rearrange("p t o -> p o t"),
+                    lower[:, :, cols].rearrange("p t o -> p o t"),
+                    ALU.max,
+                )
         hq = tile("hq", [P, O], U32)
         hq_s = tile("hq_s", [P, O], U8)
-        nc.vector.quantize_mx(out=hq[:].bitcast(E4M3), scales=hq_s[:], in_=hid[:].rearrange("p o t -> p (o t)"))
+        for c in range(2):
+            cols = slice(half * c, half * (c + 1))
+            nc.vector.quantize_mx(
+                out=hq[:, cols].bitcast(E4M3), scales=hq_s[:, cols], in_=hid[c][:].rearrange("p o t -> p (o t)")
+            )
 
-        x5_s = tile("x5_s", [P, O], U8)
-        nc.vector.tensor_copy(x5_s[:], xt_plane[:].indirect(l5[:]))
-        x5 = tile("x5", [P, O], U32)
-        nc.vector.tensor_copy(x5[:], xw[:].indirect(l5[:]))
         p_ps = [ps.tile([P, O], F32, name="p_ps%d" % h) for h in range(2)]
         for h in range(2):
             nc.tensor.matmul_mx(
                 out=p_ps[h][:], lhsT=wsw[:, 2 * P * h : 2 * P * (h + 1)].bitcast(E2M1),
-                lhsT_scale=w_plane[:, R + P * h : R + P * (h + 1)],
+                lhsT_scale=out_plane[:, P * h : P * (h + 1)],
                 rhs=x5[:].bitcast(E5M2), rhs_scale=x5_s[:], start=True, stop=False,
             )
         for h in range(2):
             nc.tensor.matmul_mx(
                 out=p_ps[h][:], lhsT=wbw[:, 2 * P * h : 2 * P * (h + 1)].bitcast(E2M1),
-                lhsT_scale=w_plane[:, R + N + P * h : R + N + P * (h + 1)],
+                lhsT_scale=out_plane[:, N + P * h : N + P * (h + 1)],
                 rhs=hq[:].bitcast(E4M3), rhs_scale=hq_s[:], start=False, stop=True,
             )
         p_sb = [tile("p_sb%d" % h, [P, O], F32) for h in range(2)]
         res = [tile("res%d" % h, [P, E], F32) for h in range(2)]
         nc.vector.tensor_copy(p_sb[0][:], p_ps[0][:])
-        nc.vector.tensor_copy(p_sb[1][:], p_ps[1][:])
-        nc.vector.tensor_copy(pages[0][0][:].indirect(l6[:]), p_sb[0][:])
-        nc.scalar.activation(pages[0][1][:].indirect(l7[:]), p_sb[0][:], COPY)
-        nc.vector.tensor_copy(pages[1][0][:].indirect(l6[:, 0:4]), p_sb[1][:, 0:64])
-        nc.scalar.activation(pages[1][1][:].indirect(l7[:]), p_sb[1][:], COPY)
-        nc.scalar.activation(pages[1][0][:].indirect(l6[:, 4:8]), p_sb[1][:, 64:128], COPY)
-        for h, c0, c1 in ((0, 0, E), (1, 0, E // 2), (1, E // 2, E)):
-            nc.vector.tensor_tensor(res[h][:, c0:c1], pages[h][0][:, c0:c1], pages[h][1][:, c0:c1], ALU.add)
-            nc.sync.dma_start(out=out[P * h : P * (h + 1), c0:c1], in_=res[h][:, c0:c1])
+        nc.scalar.activation(p_sb[1][:], p_ps[1][:], COPY)
+        for h in range(2):
+            nc.vector.tensor_copy(pages[h][0][:].indirect(l6[:]), p_sb[h][:])
+            nc.scalar.activation(pages[h][1][:].indirect(l7[:]), p_sb[h][:], COPY)
+        for h in range(2):
+            for c0 in (0, E // 2):
+                cols = slice(c0, c0 + E // 2)
+                nc.vector.tensor_tensor(res[h][:, cols], pages[h][0][:, cols], pages[h][1][:, cols], ALU.add)
+                nc.sync.dma_start(out=out[P * h : P * (h + 1), cols], in_=res[h][:, cols])

from contextlib import ExitStack

import concourse.mybir as mybir

K, T, J, R, X, O, N, E = 512, 1024, 256, 512, 1024, 128, 256, 512
FLOPS = 2 * K * R * J + 2 * R * N * O + 2 * K * N * O

F32 = mybir.dt.float32
BF16 = mybir.dt.bfloat16
I32 = mybir.dt.int32
U32 = mybir.dt.uint32
U16 = mybir.dt.uint16
U8 = mybir.dt.uint8
E4M3 = mybir.dt.float8_e4m3fn_x4
E5M2 = mybir.dt.float8_e5m2_x4
E2M1 = mybir.dt.float4_e2m1fn_x4
COPY = mybir.ActivationFunctionType.Copy
ALU = mybir.AluOpType

P = 128
PACK = 4
QUADS = 4


def tile_list_leadbounds_solo_further_pagetwice_kernel(
    tc, xt_words, xt_scales, w_words, w_scales, tb, wb_words, wb_scales, ws_words, ws_scales,
    offs, offs2, offs3, offs4, offs5, offs6, offs7, out,
):
    nc = tc.nc
    with ExitStack() as ctx:
        sb = ctx.enter_context(tc.tile_pool(name="sb", bufs=1))
        ps = ctx.enter_context(tc.psum_pool(name="ps", bufs=1))

        def tile(name, shape, dtype):
            return sb.tile(shape, dtype, name=name, align_bytes=64)

        def load_list(name, src):
            t = tile(name, list(src.shape), U16)
            nc.sync.dma_start(t[:], src)
            return t

        xt_plane = tile("xt_plane", [P, T], U8)
        w_plane = tile("w_plane", [P, R], U8)
        out_plane = tile("out_plane", [P, 2 * N], U8)
        nc.vector.memset(xt_plane[:].bitcast(I32), 0)
        nc.vector.memset(w_plane[:].bitcast(I32), 0)
        nc.vector.memset(out_plane[:].bitcast(I32), 0)
        pages = [[tile("page%d%d" % (h, s), [P, E], F32) for s in range(2)] for h in range(2)]
        for h in range(2):
            for s in range(2):
                nc.vector.memset(pages[h][s][:].bitcast(I32), 0)

        def load_rows(plane, scales, q):
            nc.sync.dma_start(
                out=plane[32 * q : 32 * q + 4, :].bitcast(I32), in_=scales[0, 4 * q : 4 * q + 4, :].bitcast(I32)
            )

        stage = tile("stage", [PACK, QUADS, R // 4], I32)
        nc.sync.dma_start(out=stage[:], in_=w_scales[0].bitcast(I32).rearrange("(q r) c -> r q c", r=4))
        l1 = load_list("l1", offs)
        xw = tile("xw", [P, T], U32)
        nc.sync.dma_start(out=xw[:].bitcast(I32), in_=xt_words[0].rearrange("p n t -> p (n t)").bitcast(I32))
        ww = tile("ww", [P, 2 * R], U8)
        nc.sync.dma_start(out=ww[:].bitcast(I32), in_=w_words[0].bitcast(I32))
        for q in range(QUADS):
            load_rows(xt_plane[:], xt_scales, q)
        tb_rows = tb.rearrange("(p t) x -> t p x", t=PACK)
        tbt = [tile("tb%d" % t, [P, X], F32) for t in range(PACK)]
        nc.sync.dma_start(out=tbt[0][:], in_=tb_rows[0])
        l5 = load_list("l5", offs5)
        nc.sync.dma_start(out=tbt[1][:], in_=tb_rows[1])
        l3 = load_list("l3", offs3)
        l4 = load_list("l4", offs4)
        l2 = load_list("l2", offs2)
        wsw = tile("wsw", [P, 2 * N], U8)
        wbw = tile("wbw", [P, 2 * N], U8)
        nc.sync.dma_start(out=wsw[:].bitcast(I32), in_=ws_words[0].bitcast(I32))
        nc.sync.dma_start(out=wbw[:].bitcast(I32), in_=wb_words[0].bitcast(I32))
        nc.sync.dma_start(out=tbt[2][:], in_=tb_rows[2])
        load_rows(out_plane[:, :N], ws_scales, 0)
        nc.sync.dma_start(out=tbt[3][:], in_=tb_rows[3])
        for q in range(1, QUADS):
            load_rows(out_plane[:, :N], ws_scales, q)
        for q in range(QUADS):
            load_rows(out_plane[:, N:], wb_scales, q)
        l6 = load_list("l6", offs6)
        l7 = load_list("l7", offs7)

        wd = [tile("wd%d" % t, [P, 2 * P], U8) for t in range(PACK)]
        for t in range(PACK):
            nc.scalar.copy(
                out=wd[t][:].bitcast(U16), in_=ww[:].bitcast(U16).rearrange("p (m t) -> p t m", t=PACK)[:, t, :]
            )
        for q in (1, 2, 3, 0):
            nc.vector.tensor_copy(w_plane[32 * q : 32 * q + 4, :].bitcast(I32), stage[:, q, :])
        xg = tile("xg", [P, J], U32)
        nc.vector.tensor_copy(xg[:], xw[:].indirect(l1[:]))
        xg_s = tile("xg_s", [P, J], U8)
        nc.vector.tensor_copy(xg_s[:], xt_plane[:].indirect(l1[:]))
        wd_s = [tile("wd_s%d" % t, [P, P], U8) for t in range(PACK)]
        a_ps = [ps.tile([P, J], F32, name="a_ps%d" % t) for t in range(PACK)]
        for t in range(PACK):
            nc.vector.tensor_copy(wd_s[t][:], w_plane[:, :R].rearrange("p (m t) -> p t m", t=PACK)[:, t, :])
            nc.tensor.matmul_mx(
                out=a_ps[t][:], lhsT=wd[t][:].bitcast(E2M1), lhsT_scale=wd_s[t][:],
                rhs=xg[:].bitcast(E5M2), rhs_scale=xg_s[:], start=True, stop=True,
            )

        x5_s = tile("x5_s", [P, O], U8)
        nc.vector.tensor_copy(x5_s[:], xt_plane[:].indirect(l5[:]))
        x5 = tile("x5", [P, O], U32)
        nc.vector.tensor_copy(x5[:], xw[:].indirect(l5[:]))

        groups = [(0, 2), (2, 4)]
        half = O // 2
        hid = [tile("hid%d" % c, [P, half, PACK], BF16) for c in range(2)]
        for t0, t1 in groups:
            n_t = t1 - t0
            picked = tile("picked%d" % t0, [P, n_t, O], F32)
            upper = tile("upper%d" % t0, [P, n_t, O], F32)
            lower = tile("lower%d" % t0, [P, n_t, O], F32)
            cut = tile("cut%d" % t0, [P, n_t, O], F32)
            for t in range(t0, t1):
                a_sb = tile("a_sb%d" % t, [P, J], F32)
                if t < 2:
                    nc.scalar.activation(a_sb[:], a_ps[t][:], COPY)
                else:
                    nc.vector.tensor_copy(a_sb[:], a_ps[t][:])
                nc.scalar.activation(upper[:, t - t0, :], tbt[t][:].indirect(l3[:]), COPY, scale=a_sb[:, 0:1])
                nc.scalar.activation(lower[:, t - t0, :], tbt[t][:].indirect(l4[:]), COPY, scale=a_sb[:, 128:129])
                nc.vector.tensor_copy(picked[:, t - t0, :], a_sb[:].indirect(l2[:]))
                if t0 > 0:
                    nc.vector.tensor_tensor(cut[:, t - t0, :], picked[:, t - t0, :], upper[:, t - t0, :], ALU.min)
            if t0 == 0:
                nc.vector.tensor_tensor(cut[:], picked[:], upper[:], ALU.min)
            for c in range(2):
                cols = slice(half * c, half * (c + 1))
                nc.vector.tensor_tensor(
                    hid[c][:, :, t0:t1],
                    cut[:, :, cols].rearrange("p t o -> p o t"),
                    lower[:, :, cols].rearrange("p t o -> p o t"),
                    ALU.max,
                )
        hq = tile("hq", [P, O], U32)
        hq_s = tile("hq_s", [P, O], U8)
        for c in range(2):
            cols = slice(half * c, half * (c + 1))
            nc.vector.quantize_mx(
                out=hq[:, cols].bitcast(E4M3), scales=hq_s[:, cols], in_=hid[c][:].rearrange("p o t -> p (o t)")
            )

        p_ps = [ps.tile([P, O], F32, name="p_ps%d" % h) for h in range(2)]
        for h in range(2):
            nc.tensor.matmul_mx(
                out=p_ps[h][:], lhsT=wsw[:, 2 * P * h : 2 * P * (h + 1)].bitcast(E2M1),
                lhsT_scale=out_plane[:, P * h : P * (h + 1)],
                rhs=x5[:].bitcast(E5M2), rhs_scale=x5_s[:], start=True, stop=False,
            )
        for h in range(2):
            nc.tensor.matmul_mx(
                out=p_ps[h][:], lhsT=wbw[:, 2 * P * h : 2 * P * (h + 1)].bitcast(E2M1),
                lhsT_scale=out_plane[:, N + P * h : N + P * (h + 1)],
                rhs=hq[:].bitcast(E4M3), rhs_scale=hq_s[:], start=False, stop=True,
            )
        p_sb = [tile("p_sb%d" % h, [P, O], F32) for h in range(2)]
        res = [tile("res%d" % h, [P, E], F32) for h in range(2)]
        nc.vector.tensor_copy(p_sb[0][:], p_ps[0][:])
        nc.scalar.activation(p_sb[1][:], p_ps[1][:], COPY)
        for h in range(2):
            nc.vector.tensor_copy(pages[h][0][:].indirect(l6[:]), p_sb[h][:])
            nc.scalar.activation(pages[h][1][:].indirect(l7[:]), p_sb[h][:], COPY)
        for h in range(2):
            for c0 in (0, E // 2):
                cols = slice(c0, c0 + E // 2)
                nc.vector.tensor_tensor(res[h][:, cols], pages[h][0][:, cols], pages[h][1][:, cols], ALU.add)
                nc.sync.dma_start(out=out[P * h : P * (h + 1), cols], in_=res[h][:, cols])
